import numpy as np
import ml_dtypes


def mxq(x, axis, fmt="e4m3"):
    dtype, down = {"e4m3": (ml_dtypes.float8_e4m3fn, 7), "e5m2": (ml_dtypes.float8_e5m2, 14)}[fmt]
    v = np.moveaxis(np.asarray(x, np.float32).astype(ml_dtypes.bfloat16).astype(np.float64), axis, -1)
    blocks = v.reshape(v.shape[:-1] + (-1, 32))
    amax = np.abs(blocks).max(-1, keepdims=True)
    byte = np.maximum(np.where(amax > 0, np.frexp(amax)[1] - 1 + 127, 0) - down, 1)
    scale = np.exp2(byte - 127.0)
    codes = (blocks / scale).astype(np.float32).astype(dtype).astype(np.float64)
    return np.moveaxis((codes * scale).reshape(v.shape), -1, axis)


WIDE = False


def mx_kscale(k):
    if not WIDE:
        return np.ones(k)
    levels = np.array([10, -10, 5, -5, 0])
    if k % 512:
        return np.exp2(np.random.permutation(np.resize(levels, k // 32))).repeat(32)
    a = np.empty((k // 512, 16))
    for p in range(k // 512):
        a[p, :8] = np.random.permutation(np.resize(levels, 8))
        for g in range(8):
            far = levels[np.abs(levels - a[p, g]) >= 10]
            a[p, g + 8] = far[np.random.randint(len(far))]
    return np.exp2(a.ravel()).repeat(32)


def f64(x):
    return np.asarray(x).astype(np.float64)


def striped(idx):
    return np.tile(idx.reshape(-1, 16).T, (8, 1)).astype(np.uint16)


def unstriped(offs):
    return offs[:16].T.reshape(-1).astype(np.int64)


E2M1 = np.array([0.0, 0.5, 1.0, 1.5, 2.0, 3.0, 4.0, 6.0, -0.0, -0.5, -1.0, -1.5, -2.0, -3.0, -4.0, -6.0])


def pack_weight(w, fmt):
    k, n = w.shape
    w = f64(np.asarray(w, np.float32).astype(ml_dtypes.bfloat16)).reshape(k // 32, 32, n)
    amax = np.abs(w).max(1)
    if fmt == "e4m3":
        byte = np.frexp(amax)[1] - 1 + 127 - 7
    else:
        mant, ex = np.frexp(amax / 6.0)
        byte = np.where(mant > 0.5, ex, ex - 1) + 127
    byte = np.clip(np.where(amax > 0, byte, 1), 1, 254)
    scaled = (w * np.exp2(127.0 - byte)[:, None, :]).reshape(k, n).astype(np.float32)
    by_word = np.ascontiguousarray(scaled.reshape(k // 512, 128, 4, n).transpose(0, 1, 3, 2))
    if fmt == "e4m3":
        words = by_word.astype(ml_dtypes.float8_e4m3fn).view(np.uint8)
    else:
        c = by_word.astype(ml_dtypes.float4_e2m1fn).view(np.uint8) & 0xF
        words = (c[..., 0::2] | (c[..., 1::2] << 4)).reshape(k // 512, 128, 2 * n)
    return np.ascontiguousarray(words), np.ascontiguousarray(byte.astype(np.uint8).reshape(k // 512, 16, n))


def unpack_weight(words, scales, fmt):
    g, _, n = scales.shape
    words = np.ascontiguousarray(words).reshape(g, 128, n, -1)
    if fmt == "e4m3":
        vals = words.view(ml_dtypes.float8_e4m3fn).astype(np.float64)
    else:
        nib = np.empty((g, 128, n, 4), np.uint8)
        nib[..., 0::2] = words & 0xF
        nib[..., 1::2] = words >> 4
        vals = E2M1[nib]
    vals = vals * np.repeat(np.exp2(scales.astype(np.float64) - 127.0), 8, axis=1)[..., None]
    return vals.transpose(0, 1, 3, 2).reshape(g * 512, n)


def gelu(v):
    return 0.5 * v * (1.0 + np.tanh(np.sqrt(2.0 / np.pi) * (v + 0.044715 * v**3)))


K, T, E, C, N = 1024, 768, 12, 128, 256
TOP = 4
PAD = 64


def by_expert(wq, xq):
    return np.concatenate([wq[e].T @ xq[:, e * C:(e + 1) * C] for e in range(E)], axis=1)


def setup_inputs():
    n = np.random.standard_normal
    s = mx_kscale(K)[:, None]
    slot_token = np.empty(E * C, np.int64); pos = np.tile(E * C + np.arange(T) % PAD, (TOP, 1)); taken = np.zeros(T, np.int64)
    liked = np.random.randn(T)
    for e in np.random.permutation(E):
        free = np.flatnonzero(taken < TOP); pick = np.random.permutation(free[np.argsort(-(liked[free] + np.random.gumbel(size=free.size)))[:C]]); slot_token[e * C:(e + 1) * C] = pick
        pos[taken[pick], pick] = e * C + np.arange(C); taken[pick] += 1
    g = np.random.uniform(0.2, 0.8, (TOP, T))
    w = [pack_weight(m, "e2m1") for m in n((E, K, N)) / np.sqrt(K) / s[None]]
    return {
        "xT": (n((K, T)) * s).astype(np.float32),
        "w_words": np.stack([m[0] for m in w]),
        "w_scales": np.stack([m[1] for m in w]),
        "b": (0.3 * n((N, E))).astype(np.float32),
        "gate": np.stack([np.tile(r, (N, 1)) for r in g]).astype(np.float32),
        "offs": striped(slot_token),
        "pos1": striped(pos[0]),
        "pos2": striped(pos[1]),
        "pos3": striped(pos[2]),
        "pos4": striped(pos[3]),
    }


def reference(xT, w_words, w_scales, b, gate, offs, pos1, pos2, pos3, pos4):
    idx = unstriped(offs)
    w = np.stack([unpack_weight(w_words[e], w_scales[e], "e2m1") for e in range(E)])
    xq = mxq(f64(xT)[:, idx], 0, "e4m3")
    y = by_expert(w, xq)
    y = gelu(y + np.repeat(f64(b), C, axis=1))
    y = np.concatenate([y, np.zeros((N, PAD))], axis=1)
    return sum(f64(gate[r]) * y[:, unstriped(p)] for r, p in enumerate((pos1, pos2, pos3, pos4)))

@@ -1,0 +1,257 @@
+from contextlib import ExitStack
+
+import concourse.mybir as mybir
+from concourse.masks import make_identity
+
+K, T, E, C, N = 1024, 768, 12, 128, 256
+TOP = 4
+PAD = 64
+S = E * C
+P = 128
+PASSES = K // 512
+HALVES = N // P
+FLOPS = 2 * K * N * S
+BYTES = 4 * K * T + E * K * N // 2 + E * K * N // 32 + 4 * N * E + 4 * TOP * T + 2 * 128 * (S + TOP * T) // 16 + 4 * N * T
+
+F32 = mybir.dt.float32
+BF16 = mybir.dt.bfloat16
+I32 = mybir.dt.int32
+U32 = mybir.dt.uint32
+U16 = mybir.dt.uint16
+U8 = mybir.dt.uint8
+FP8X4 = mybir.dt.float8_e4m3fn_x4
+FP4X4 = mybir.dt.float4_e2m1fn_x4
+COPY = mybir.ActivationFunctionType.Copy
+GELU = mybir.ActivationFunctionType.Gelu_apprx_tanh
+
+X_CHUNKS = (((0, 256), (256, 512), (512, 768)), ((0, 256), (256, 512), (512, 768)))
+GROUPS = ((0, 4), (4, 8), (8, 12))
+LAST_GROUPS = ((0, 4), (4, 8), (8, 11), (11, 12))
+TB = 384
+
+
+def tile_moe_ecr_lin_gelu_kernel(tc, xT, w_words, w_scales, b, gate, offs, pos1, pos2, pos3, pos4, out):
+    nc = tc.nc
+    with ExitStack() as ctx:
+        keep = ctx.enter_context(tc.tile_pool(name="keep", bufs=1))
+        ring = ctx.enter_context(tc.tile_pool(name="ring", bufs=3))
+        psum = ctx.enter_context(tc.psum_pool(name="psum", bufs=1))
+
+        def bank(i, name):
+            return psum.tile([P, 512], F32, tag="bank%d" % i, name=name)
+
+        w_plane = keep.tile([P, E * PASSES * N], U8, align_bytes=64, name="w_plane")
+        nc.vector.memset(w_plane[:].bitcast(I32), 0)
+        x_plane = keep.tile([P, T], U8, align_bytes=64, name="x_plane")
+        nc.vector.memset(x_plane[:].bitcast(I32), 0)
+        shifted = []
+        for g in range(len(GROUPS)):
+            t = keep.tile([P, 512], U8, align_bytes=64, name="shifted%d" % g)
+            nc.vector.memset(t[:].bitcast(I32), 0)
+            shifted.append(t)
+        gate_rows = keep.tile([P, T], F32, name="gate_rows")
+        nc.gpsimd.memset(gate_rows[:], 0.0)
+        nc.gpsimd.dma_start(out=gate_rows[0:TOP, :], in_=gate[:, 0, :])
+        bias = keep.tile([P, HALVES, E], F32, name="bias")
+        nc.gpsimd.dma_start(out=bias[:], in_=b.rearrange("(h p) e -> p h e", p=P))
+        zeros = keep.tile([P, PAD], F32, name="zeros")
+        nc.vector.memset(zeros[:], 0.0)
+        ident = keep.tile([P, P], F32, name="ident")
+        make_identity(nc, ident[:])
+        y = []
+        for h in range(HALVES):
+            t = keep.tile([P, S + PAD], F32, name="y%d" % h)
+            nc.scalar.activation(out=t[:, S:], in_=zeros[:], func=GELU)
+            y.append(t)
+
+        raw = {}
+
+        def load_x(a, t0, t1):
+            t = keep.tile([P, 4, t1 - t0], F32, name="raw%d_%d" % (a, t0))
+            nc.sync.dma_start(out=t[:], in_=xT[512 * a : 512 * (a + 1), t0:t1].rearrange("(p j) t -> p j t", j=4))
+            raw[(a, t0)] = t
+
+        for t0, t1 in X_CHUNKS[0]:
+            load_x(0, t0, t1)
+        offs_t = keep.tile([P, S // 16], U16, name="offs_t")
+        nc.sync.dma_start(offs_t[:], offs)
+        for t0, t1 in X_CHUNKS[1]:
+            load_x(1, t0, t1)
+        scale_rows = w_scales.rearrange("e a q n -> q (e a) n")
+        for r in range(4):
+            nc.sync.dma_start(
+                out=w_plane[r:P:32, :].bitcast(I32).rearrange("q (g n) -> q g n", n=N // 4),
+                in_=scale_rows[r:16:4].bitcast(I32),
+            )
+        w_codes = []
+        for e0, e1 in GROUPS:
+            t = keep.tile([P, (e1 - e0) * PASSES, 2 * N], U8, align_bytes=64, name="w_codes%d" % e0)
+            nc.sync.dma_start(out=t[:].bitcast(I32), in_=w_words[e0:e1].rearrange("e a p c -> p (e a) c").bitcast(I32))
+            w_codes.append(t)
+        pos_t = []
+        for r, pos in enumerate((pos1, pos2, pos3, pos4)):
+            t = keep.tile([P, T // 16], U16, name="pos_t%d" % r)
+            nc.sync.dma_start(t[:], pos)
+            pos_t.append(t)
+
+        x_words = [keep.tile([P, T], U32, align_bytes=64, name="x_words%d" % a) for a in range(PASSES)]
+        woven = {}
+
+        def weave(a, t0, t1, on_vector):
+            t = keep.tile([P, (t1 - t0) * 4], BF16, align_bytes=64, name="woven%d_%d" % (a, t0))
+            dst = t[:].rearrange("p (c i j) -> p c j i", i=4, j=4)
+            src = raw[(a, t0)][:].rearrange("p j (c i) -> p c j i", i=4)
+            if on_vector:
+                nc.vector.tensor_copy(out=dst, in_=src)
+            else:
+                nc.scalar.activation(out=dst, in_=src, func=COPY)
+            woven[(a, t0)] = t
+
+        def quantise(a, t0, t1):
+            nc.vector.quantize_mx(
+                out=x_words[a][:, t0:t1].bitcast(FP8X4),
+                scales=x_plane[4 * (1 - a) : P, t0:t1],
+                in_=woven[(a, t0)][:],
+            )
+
+        for t0, t1 in X_CHUNKS[0]:
+            weave(0, t0, t1, True)
+            quantise(0, t0, t1)
+        for t0, t1 in X_CHUNKS[1]:
+            weave(1, t0, t1, False)
+
+        def gather_slots(window, e0, e1, dtype, name):
+            t = keep.tile([P, (e1 - e0) * C], dtype, align_bytes=64, name=name)
+            nc.vector.tensor_copy(t[:], window[:].indirect(offs_t[:, e0 * C // 16 : e1 * C // 16]))
+            return t
+
+        words0 = []
+        for g, (e0, e1) in enumerate(GROUPS):
+            words0.append(gather_slots(x_words[0], e0, e1, U32, "words0_%d" % e0))
+            quantise(1, *X_CHUNKS[1][g])
+        planes = []
+        for g, (e0, e1) in enumerate(GROUPS):
+            t = gather_slots(x_plane, e0, e1, U8, "planes%d" % e0)
+            nc.sync.dma_start(out=shifted[g][0:112, :].bitcast(I32), in_=t[4:116, :].bitcast(I32))
+            planes.append(t)
+
+        gate_cols = keep.tile([P, T // P, TOP], F32, name="gate_cols")
+        for i in range(2):
+            ps = bank(6 + i, "gate_ps%d" % i)
+            for c in range(3):
+                nc.tensor.transpose(ps[:, c * P : (c + 1) * P], gate_rows[:, (3 * i + c) * P : (3 * i + c + 1) * P], ident[:])
+            nc.scalar.activation(
+                out=gate_cols[:, 3 * i : 3 * i + 3, :],
+                in_=ps[:, 0 : 3 * P].rearrange("p (c n) -> p c n", n=P)[:, :, 0:TOP],
+                func=COPY,
+            )
+
+        words1 = {}
+
+        def experts(h, e0, e1, ps):
+            for e in range(e0, e1):
+                g, i = divmod(e, 4)
+                cols = slice(i * C, (i + 1) * C)
+                tile1, j = words1[e]
+                operands = (
+                    (1, tile1[:, j * C : (j + 1) * C], planes[g][:, cols]),
+                    (0, words0[g][:, cols], shifted[g][:, cols]),
+                )
+                for step, (a, words, plane) in enumerate(operands):
+                    n0 = (e * PASSES + a) * N + h * P
+                    nc.tensor.matmul_mx(
+                        out=ps[:, (e - e0) * C : (e - e0 + 1) * C],
+                        lhsT=w_codes[g][:, i * PASSES + a, 2 * P * h : 2 * P * (h + 1)].bitcast(FP4X4),
+                        lhsT_scale=w_plane[:, n0 : n0 + P],
+                        rhs=words.bitcast(FP8X4),
+                        rhs_scale=plane,
+                        start=(step == 0),
+                        stop=(step == 1),
+                    )
+
+        def activate(h, e0, e1, ps):
+            for e in range(e0, e1):
+                nc.scalar.activation(
+                    out=y[h][:, e * C : (e + 1) * C],
+                    in_=ps[:, (e - e0) * C : (e - e0 + 1) * C],
+                    func=GELU,
+                    bias=bias[:, h, e : e + 1],
+                )
+
+        late = []
+        for g, (e0, e1) in enumerate(LAST_GROUPS):
+            t = gather_slots(x_words[1], e0, e1, U32, "words1_%d" % e0)
+            for e in range(e0, e1):
+                words1[e] = (t, e - e0)
+            ps = bank((0, 1, 2, 6)[g], "h0_%d" % e0)
+            experts(0, e0, e1, ps)
+            activate(0, e0, e1, ps)
+            if g < 2:
+                ps = bank(3 + g, "h1_%d" % e0)
+                experts(1, e0, e1, ps)
+                late.append((e0, e1, ps))
+        ps = bank(5, "h1_8")
+        experts(1, 8, 12, ps)
+        late.append((8, 12, ps))
+
+        steps = [(h, r, u) for h in range(HALVES) for r in range(TOP) for u in range(T // TB)]
+        sums = {}
+        picked = {}
+        scaled = {}
+
+        def fetch(h, r, u):
+            if h == HALVES - 1 and r == TOP - 1:
+                t = keep.tile([P, TB], F32, name="picked_last%d" % u)
+                nc.vector.tensor_copy(t[:], y[h][:].indirect(pos_t[r][:, u * TB // 16 : (u + 1) * TB // 16]))
+                picked[(h, r, u)] = t[:]
+            elif u == 0:
+                t = ring.tile([P, T], F32, name="picked")
+                nc.vector.tensor_copy(t[:], y[h][:].indirect(pos_t[r][:]))
+                for v in range(T // TB):
+                    picked[(h, r, v)] = t[:, v * TB : (v + 1) * TB]
+
+        def turn_and_scale(i):
+            h, r, u = steps[i]
+            ps = bank((7, 0, 1)[i % 3], "turned%d" % i)
+            for c in range(TB // P):
+                nc.tensor.transpose(ps[:, c * P : (c + 1) * P], picked[(h, r, u)][:, c * P : (c + 1) * P], ident[:])
+            t = ring.tile([P, TB], F32, name="scaled")
+            for c in range(TB // P):
+                nc.scalar.activation(
+                    out=t[:, c * P : (c + 1) * P],
+                    in_=ps[:, c * P : (c + 1) * P],
+                    func=COPY,
+                    scale=gate_cols[:, u * (TB // P) + c, r : r + 1],
+                )
+            scaled[i] = t
+
+        def turn_back(i):
+            h, r, u = steps[i]
+            if r == 0:
+                sums[(h, u)] = bank(((2, 6), (3, 4))[h][u], "sum%d_%d" % (h, u))
+            ps = sums[(h, u)]
+            for c in range(TB // P):
+                nc.tensor.matmul(
+                    ps[:, c * P : (c + 1) * P],
+                    lhsT=scaled[i][:, c * P : (c + 1) * P],
+                    rhs=ident[:],
+                    is_transpose=True,
+                    start=(r == 0 and c == 0),
+                    stop=(r == TOP - 1 and c == TB // P - 1),
+                )
+            if r == TOP - 1:
+                t = keep.tile([P, TB], F32, name="result%d_%d" % (h, u))
+                if h == HALVES - 1:
+                    nc.vector.tensor_copy(out=t[:], in_=ps[:, 0:TB])
+                else:
+                    nc.scalar.copy(out=t[:], in_=ps[:, 0:TB])
+                nc.sync.dma_start(out=out[h * P : (h + 1) * P, u * TB : (u + 1) * TB], in_=t[:])
+
+        for i, (h, r, u) in enumerate(steps):
+            fetch(h, r, u)
+            if i < 2 * len(late) and i % 2 == 0:
+                activate(1, *late[i // 2])
+            turn_and_scale(i)
+            if i > 0:
+                turn_back(i - 1)
+        turn_back(len(steps) - 1)

@@ -26,20 +26,26 @@ GELU = mybir.ActivationFunctionType.Gelu_apprx_tanh
 
 X_CHUNKS = (((0, 256), (256, 512), (512, 768)), ((0, 256), (256, 512), (512, 768)))
 GROUPS = ((0, 4), (4, 8), (8, 12))
-LAST_GROUPS = ((0, 4), (4, 8), (8, 11), (11, 12))
-TB = 384
+LAST_GROUPS = ((0, 2), (2, 4), (4, 6), (6, 8), (8, 10), (10, 11), (11, 12))
+PIECES = ((0, 512), (512, 768))
+LAG = 2
 
 
 def tile_moe_ecr_lin_gelu_kernel(tc, xT, w_words, w_scales, b, gate, offs, pos1, pos2, pos3, pos4, out):
     nc = tc.nc
     with ExitStack() as ctx:
         keep = ctx.enter_context(tc.tile_pool(name="keep", bufs=1))
-        ring = ctx.enter_context(tc.tile_pool(name="ring", bufs=3))
+        ring = ctx.enter_context(tc.tile_pool(name="ring", bufs=4))
         psum = ctx.enter_context(tc.psum_pool(name="psum", bufs=1))
 
         def bank(i, name):
             return psum.tile([P, 512], F32, tag="bank%d" % i, name=name)
 
+        gate_rows = keep.tile([P, T], F32, name="gate_rows")
+        nc.vector.memset(gate_rows[:], 0.0)
+        bias = keep.tile([P, HALVES, E], F32, name="bias")
+        nc.scalar.dma_start(out=bias[:], in_=b.rearrange("(h p) e -> p h e", p=P))
+        nc.scalar.dma_start(out=gate_rows[0:TOP, :], in_=gate[:, 0, :])
         w_plane = keep.tile([P, E * PASSES * N], U8, align_bytes=64, name="w_plane")
         nc.vector.memset(w_plane[:].bitcast(I32), 0)
         x_plane = keep.tile([P, T], U8, align_bytes=64, name="x_plane")
@@ -49,11 +55,6 @@ def tile_moe_ecr_lin_gelu_kernel(tc, xT, w_words, w_scales, b, gate, offs, pos1,
             t = keep.tile([P, 512], U8, align_bytes=64, name="shifted%d" % g)
             nc.vector.memset(t[:].bitcast(I32), 0)
             shifted.append(t)
-        gate_rows = keep.tile([P, T], F32, name="gate_rows")
-        nc.gpsimd.memset(gate_rows[:], 0.0)
-        nc.gpsimd.dma_start(out=gate_rows[0:TOP, :], in_=gate[:, 0, :])
-        bias = keep.tile([P, HALVES, E], F32, name="bias")
-        nc.gpsimd.dma_start(out=bias[:], in_=b.rearrange("(h p) e -> p h e", p=P))
         zeros = keep.tile([P, PAD], F32, name="zeros")
         nc.vector.memset(zeros[:], 0.0)
         ident = keep.tile([P, P], F32, name="ident")
@@ -84,15 +85,21 @@ def tile_moe_ecr_lin_gelu_kernel(tc, xT, w_words, w_scales, b, gate, offs, pos1,
                 in_=scale_rows[r:16:4].bitcast(I32),
             )
         w_codes = []
-        for e0, e1 in GROUPS:
+
+        def load_w(e0, e1):
             t = keep.tile([P, (e1 - e0) * PASSES, 2 * N], U8, align_bytes=64, name="w_codes%d" % e0)
             nc.sync.dma_start(out=t[:].bitcast(I32), in_=w_words[e0:e1].rearrange("e a p c -> p (e a) c").bitcast(I32))
             w_codes.append(t)
+
+        for e0, e1 in GROUPS:
+            load_w(e0, e1)
         pos_t = []
         for r, pos in enumerate((pos1, pos2, pos3, pos4)):
             t = keep.tile([P, T // 16], U16, name="pos_t%d" % r)
             nc.sync.dma_start(t[:], pos)
             pos_t.append(t)
+        gate_last = keep.tile([P, 512], F32, name="gate_last")
+        nc.sync.dma_start(out=gate_last[:], in_=gate[TOP - 1, N - P : N, 0:512])
 
         x_words = [keep.tile([P, T], U32, align_bytes=64, name="x_words%d" % a) for a in range(PASSES)]
         woven = {}
@@ -100,7 +107,8 @@ def tile_moe_ecr_lin_gelu_kernel(tc, xT, w_words, w_scales, b, gate, offs, pos1,
         def weave(a, t0, t1, on_vector):
             t = keep.tile([P, (t1 - t0) * 4], BF16, align_bytes=64, name="woven%d_%d" % (a, t0))
             dst = t[:].rearrange("p (c i j) -> p c j i", i=4, j=4)
-            src = raw[(a, t0)][:].rearrange("p j (c i) -> p c j i", i=4)
+            base = t0 - t0 % 256
+            src = raw[(a, base)][:, :, t0 - base : t1 - base].rearrange("p j (c i) -> p c j i", i=4)
             if on_vector:
                 nc.vector.tensor_copy(out=dst, in_=src)
             else:
@@ -110,13 +118,16 @@ def tile_moe_ecr_lin_gelu_kernel(tc, xT, w_words, w_scales, b, gate, offs, pos1,
         def quantise(a, t0, t1):
             nc.vector.quantize_mx(
                 out=x_words[a][:, t0:t1].bitcast(FP8X4),
-                scales=x_plane[4 * (1 - a) : P, t0:t1],
+                scales=x_plane[4 * a : P, t0:t1],
                 in_=woven[(a, t0)][:],
             )
 
-        for t0, t1 in X_CHUNKS[0]:
-            weave(0, t0, t1, True)
-            quantise(0, t0, t1)
+        first = ((0, 256, True), (256, 512, False), (512, 640, True), (640, 768, False))
+        weave(0, *first[0])
+        for i in range(1, len(first)):
+            weave(0, *first[i])
+            quantise(0, *first[i - 1][:2])
+        quantise(0, *first[-1][:2])
         for t0, t1 in X_CHUNKS[1]:
             weave(1, t0, t1, False)
 
@@ -132,7 +143,7 @@ def tile_moe_ecr_lin_gelu_kernel(tc, xT, w_words, w_scales, b, gate, offs, pos1,
         planes = []
         for g, (e0, e1) in enumerate(GROUPS):
             t = gather_slots(x_plane, e0, e1, U8, "planes%d" % e0)
-            nc.sync.dma_start(out=shifted[g][0:112, :].bitcast(I32), in_=t[4:116, :].bitcast(I32))
+            nc.scalar.dma_start(out=shifted[g][0:112, :].bitcast(I32), in_=t[4:116, :].bitcast(I32))
             planes.append(t)
 
         gate_cols = keep.tile([P, T // P, TOP], F32, name="gate_cols")
@@ -148,110 +159,126 @@ def tile_moe_ecr_lin_gelu_kernel(tc, xT, w_words, w_scales, b, gate, offs, pos1,
 
         words1 = {}
 
+        def one_pass(h, e, a, acc):
+            g, i = divmod(e, 4)
+            cols = slice(i * C, (i + 1) * C)
+            words, plane = (words0[g][:, cols], planes[g][:, cols]) if a == 0 else (words1[e], shifted[g][:, cols])
+            n0 = (e * PASSES + a) * N + h * P
+            nc.tensor.matmul_mx(
+                out=acc,
+                lhsT=w_codes[g][:, i * PASSES + a, 2 * P * h : 2 * P * (h + 1)].bitcast(FP4X4),
+                lhsT_scale=w_plane[:, n0 : n0 + P],
+                rhs=words.bitcast(FP8X4),
+                rhs_scale=plane,
+                start=(a == 0),
+                stop=(a == PASSES - 1),
+            )
+
+        def activate(h, e, acc):
+            nc.scalar.activation(out=y[h][:, e * C : (e + 1) * C], in_=acc, func=GELU, bias=bias[:, h, e : e + 1])
+
         def experts(h, e0, e1, ps):
             for e in range(e0, e1):
-                g, i = divmod(e, 4)
-                cols = slice(i * C, (i + 1) * C)
-                tile1, j = words1[e]
-                operands = (
-                    (1, tile1[:, j * C : (j + 1) * C], planes[g][:, cols]),
-                    (0, words0[g][:, cols], shifted[g][:, cols]),
-                )
-                for step, (a, words, plane) in enumerate(operands):
-                    n0 = (e * PASSES + a) * N + h * P
-                    nc.tensor.matmul_mx(
-                        out=ps[:, (e - e0) * C : (e - e0 + 1) * C],
-                        lhsT=w_codes[g][:, i * PASSES + a, 2 * P * h : 2 * P * (h + 1)].bitcast(FP4X4),
-                        lhsT_scale=w_plane[:, n0 : n0 + P],
-                        rhs=words.bitcast(FP8X4),
-                        rhs_scale=plane,
-                        start=(step == 0),
-                        stop=(step == 1),
-                    )
-
-        def activate(h, e0, e1, ps):
+                for a in range(PASSES):
+                    one_pass(h, e, a, ps[:, (e - e0) * C : (e - e0 + 1) * C])
             for e in range(e0, e1):
-                nc.scalar.activation(
-                    out=y[h][:, e * C : (e + 1) * C],
-                    in_=ps[:, (e - e0) * C : (e - e0 + 1) * C],
-                    func=GELU,
-                    bias=bias[:, h, e : e + 1],
-                )
+                activate(h, e, ps[:, (e - e0) * C : (e - e0 + 1) * C])
 
-        late = []
+        opened = {}
         for g, (e0, e1) in enumerate(LAST_GROUPS):
             t = gather_slots(x_words[1], e0, e1, U32, "words1_%d" % e0)
             for e in range(e0, e1):
-                words1[e] = (t, e - e0)
-            ps = bank((0, 1, 2, 6)[g], "h0_%d" % e0)
-            experts(0, e0, e1, ps)
-            activate(0, e0, e1, ps)
-            if g < 2:
-                ps = bank(3 + g, "h1_%d" % e0)
-                experts(1, e0, e1, ps)
-                late.append((e0, e1, ps))
-        ps = bank(5, "h1_8")
-        experts(1, 8, 12, ps)
-        late.append((8, 12, ps))
+                words1[e] = t[:, (e - e0) * C : (e - e0 + 1) * C]
+            if e1 == 10:
+                for e in (10, 11):
+                    opened[e] = bank(e - 5, "h0_%d" % e)[:, 0:C]
+                    one_pass(0, e, 0, opened[e])
+            if e0 in opened:
+                one_pass(0, e0, 1, opened[e0])
+                activate(0, e0, opened[e0])
+            else:
+                experts(0, e0, e1, bank(g, "h0_%d" % e0))
+        for (e0, e1), i in zip((GROUPS[2], GROUPS[0], GROUPS[1]), (7, 6, 5)):
+            experts(1, e0, e1, bank(i, "h1_%d" % e0))
 
-        steps = [(h, r, u) for h in range(HALVES) for r in range(TOP) for u in range(T // TB)]
+        steps = [(h, r, u) for h in range(HALVES) for r in range(TOP) for u in range(len(PIECES))]
+        steps.remove((HALVES - 1, TOP - 1, 0))
         sums = {}
         picked = {}
         scaled = {}
 
         def fetch(h, r, u):
-            if h == HALVES - 1 and r == TOP - 1:
-                t = keep.tile([P, TB], F32, name="picked_last%d" % u)
-                nc.vector.tensor_copy(t[:], y[h][:].indirect(pos_t[r][:, u * TB // 16 : (u + 1) * TB // 16]))
+            t0, t1 = PIECES[u]
+            if h == HALVES - 1 and r >= TOP - 2:
+                t = ring.tile([P, t1 - t0], F32, tag="picked", name="picked_piece")
+                nc.vector.tensor_copy(t[:], y[h][:].indirect(pos_t[r][:, t0 // 16 : t1 // 16]))
                 picked[(h, r, u)] = t[:]
             elif u == 0:
-                t = ring.tile([P, T], F32, name="picked")
+                t = ring.tile([P, T], F32, tag="picked", name="picked")
                 nc.vector.tensor_copy(t[:], y[h][:].indirect(pos_t[r][:]))
-                for v in range(T // TB):
-                    picked[(h, r, v)] = t[:, v * TB : (v + 1) * TB]
+                for v, (v0, v1) in enumerate(PIECES):
+                    picked[(h, r, v)] = t[:, v0:v1]
 
         def turn_and_scale(i):
             h, r, u = steps[i]
-            ps = bank((7, 0, 1)[i % 3], "turned%d" % i)
-            for c in range(TB // P):
-                nc.tensor.transpose(ps[:, c * P : (c + 1) * P], picked[(h, r, u)][:, c * P : (c + 1) * P], ident[:])
-            t = ring.tile([P, TB], F32, name="scaled")
-            for c in range(TB // P):
+            t0, t1 = PIECES[u]
+            blocks = (t1 - t0) // P
+            if i < len(steps) - 1:
+                ps = bank(i % 3, "turned%d" % i)
+                turned = [ps[:, c * P : (c + 1) * P] for c in range(blocks)]
+            else:
+                turned = [bank(3 + c, "turned_last%d" % c)[:, 0:P] for c in range(blocks)]
+            for c in range(blocks):
+                nc.tensor.transpose(turned[c], picked[(h, r, u)][:, c * P : (c + 1) * P], ident[:])
+            t = ring.tile([P, t1 - t0], F32, tag="scaled", name="scaled")
+            for c in range(blocks):
                 nc.scalar.activation(
                     out=t[:, c * P : (c + 1) * P],
-                    in_=ps[:, c * P : (c + 1) * P],
+                    in_=turned[c],
                     func=COPY,
-                    scale=gate_cols[:, u * (TB // P) + c, r : r + 1],
+                    scale=gate_cols[:, t0 // P + c, r : r + 1],
                 )
             scaled[i] = t
 
+        def store(h, t0, t1, t):
+            nc.sync.dma_start(out=out[h * P : (h + 1) * P, t0:t1], in_=t[:])
+
         def turn_back(i):
             h, r, u = steps[i]
+            t0, t1 = PIECES[u]
+            blocks = (t1 - t0) // P
             if r == 0:
-                sums[(h, u)] = bank(((2, 6), (3, 4))[h][u], "sum%d_%d" % (h, u))
+                sums[(h, u)] = bank(((3, 4), (6, 5))[h][u], "sum%d_%d" % (h, u))
             ps = sums[(h, u)]
-            for c in range(TB // P):
+            last = TOP - 2 if (h, u) == (HALVES - 1, 0) else TOP - 1
+            for c in range(blocks):
                 nc.tensor.matmul(
                     ps[:, c * P : (c + 1) * P],
                     lhsT=scaled[i][:, c * P : (c + 1) * P],
                     rhs=ident[:],
                     is_transpose=True,
                     start=(r == 0 and c == 0),
-                    stop=(r == TOP - 1 and c == TB // P - 1),
+                    stop=(r == last and c == blocks - 1),
                 )
             if r == TOP - 1:
-                t = keep.tile([P, TB], F32, name="result%d_%d" % (h, u))
-                if h == HALVES - 1:
-                    nc.vector.tensor_copy(out=t[:], in_=ps[:, 0:TB])
-                else:
-                    nc.scalar.copy(out=t[:], in_=ps[:, 0:TB])
-                nc.sync.dma_start(out=out[h * P : (h + 1) * P, u * TB : (u + 1) * TB], in_=t[:])
+                t = keep.tile([P, t1 - t0], F32, name="result%d_%d" % (h, u))
+                nc.scalar.copy(out=t[:], in_=ps[:, 0 : t1 - t0])
+                store(h, t0, t1, t)
 
         for i, (h, r, u) in enumerate(steps):
             fetch(h, r, u)
-            if i < 2 * len(late) and i % 2 == 0:
-                activate(1, *late[i // 2])
             turn_and_scale(i)
-            if i > 0:
-                turn_back(i - 1)
-        turn_back(len(steps) - 1)
+            if i >= LAG:
+                turn_back(i - LAG)
+        product = ring.tile([P, 512], F32, tag="picked", name="product")
+        nc.vector.tensor_tensor(
+            product[:], y[HALVES - 1][:].indirect(pos_t[TOP - 1][:, 0 : 512 // 16]), gate_last[:], mybir.AluOpType.mult
+        )
+        for t0 in (0, 256):
+            total = keep.tile([P, 256], F32, name="total%d" % t0)
+            nc.vector.tensor_tensor(
+                total[:], sums[(HALVES - 1, 0)][:, t0 : t0 + 256], product[:, t0 : t0 + 256], mybir.AluOpType.add
+            )
+            store(HALVES - 1, t0, t0 + 256, total)
+        for i in range(len(steps) - LAG, len(steps)):
+            turn_back(i)

from contextlib import ExitStack

import concourse.mybir as mybir
from concourse.masks import make_identity

K, T, E, C, N = 1024, 768, 12, 128, 256
TOP = 4
PAD = 64
S = E * C
P = 128
PASSES = K // 512
HALVES = N // P
FLOPS = 2 * K * N * S
BYTES = 4 * K * T + E * K * N // 2 + E * K * N // 32 + 4 * N * E + 4 * TOP * T + 2 * 128 * (S + TOP * T) // 16 + 4 * N * T

F32 = mybir.dt.float32
BF16 = mybir.dt.bfloat16
I32 = mybir.dt.int32
U32 = mybir.dt.uint32
U16 = mybir.dt.uint16
U8 = mybir.dt.uint8
FP8X4 = mybir.dt.float8_e4m3fn_x4
FP4X4 = mybir.dt.float4_e2m1fn_x4
COPY = mybir.ActivationFunctionType.Copy
GELU = mybir.ActivationFunctionType.Gelu_apprx_tanh

X_CHUNKS = (((0, 256), (256, 512), (512, 768)), ((0, 256), (256, 512), (512, 768)))
GROUPS = ((0, 4), (4, 8), (8, 12))
LAST_GROUPS = ((0, 2), (2, 4), (4, 6), (6, 8), (8, 10), (10, 11), (11, 12))
PIECES = ((0, 512), (512, 768))
LAG = 2


def tile_moe_ecr_lin_gelu_kernel(tc, xT, w_words, w_scales, b, gate, offs, pos1, pos2, pos3, pos4, out):
    nc = tc.nc
    with ExitStack() as ctx:
        keep = ctx.enter_context(tc.tile_pool(name="keep", bufs=1))
        ring = ctx.enter_context(tc.tile_pool(name="ring", bufs=4))
        psum = ctx.enter_context(tc.psum_pool(name="psum", bufs=1))

        def bank(i, name):
            return psum.tile([P, 512], F32, tag="bank%d" % i, name=name)

        gate_rows = keep.tile([P, T], F32, name="gate_rows")
        nc.vector.memset(gate_rows[:], 0.0)
        bias = keep.tile([P, HALVES, E], F32, name="bias")
        nc.scalar.dma_start(out=bias[:], in_=b.rearrange("(h p) e -> p h e", p=P))
        nc.scalar.dma_start(out=gate_rows[0:TOP, :], in_=gate[:, 0, :])
        w_plane = keep.tile([P, E * PASSES * N], U8, align_bytes=64, name="w_plane")
        nc.vector.memset(w_plane[:].bitcast(I32), 0)
        x_plane = keep.tile([P, T], U8, align_bytes=64, name="x_plane")
        nc.vector.memset(x_plane[:].bitcast(I32), 0)
        shifted = []
        for g in range(len(GROUPS)):
            t = keep.tile([P, 512], U8, align_bytes=64, name="shifted%d" % g)
            nc.vector.memset(t[:].bitcast(I32), 0)
            shifted.append(t)
        zeros = keep.tile([P, PAD], F32, name="zeros")
        nc.vector.memset(zeros[:], 0.0)
        ident = keep.tile([P, P], F32, name="ident")
        make_identity(nc, ident[:])
        y = []
        for h in range(HALVES):
            t = keep.tile([P, S + PAD], F32, name="y%d" % h)
            nc.scalar.activation(out=t[:, S:], in_=zeros[:], func=GELU)
            y.append(t)

        raw = {}

        def load_x(a, t0, t1):
            t = keep.tile([P, 4, t1 - t0], F32, name="raw%d_%d" % (a, t0))
            nc.sync.dma_start(out=t[:], in_=xT[512 * a : 512 * (a + 1), t0:t1].rearrange("(p j) t -> p j t", j=4))
            raw[(a, t0)] = t

        for t0, t1 in X_CHUNKS[0]:
            load_x(0, t0, t1)
        offs_t = keep.tile([P, S // 16], U16, name="offs_t")
        nc.sync.dma_start(offs_t[:], offs)
        for t0, t1 in X_CHUNKS[1]:
            load_x(1, t0, t1)
        scale_rows = w_scales.rearrange("e a q n -> q (e a) n")
        for r in range(4):
            nc.sync.dma_start(
                out=w_plane[r:P:32, :].bitcast(I32).rearrange("q (g n) -> q g n", n=N // 4),
                in_=scale_rows[r:16:4].bitcast(I32),
            )
        w_codes = []

        def load_w(e0, e1):
            t = keep.tile([P, (e1 - e0) * PASSES, 2 * N], U8, align_bytes=64, name="w_codes%d" % e0)
            nc.sync.dma_start(out=t[:].bitcast(I32), in_=w_words[e0:e1].rearrange("e a p c -> p (e a) c").bitcast(I32))
            w_codes.append(t)

        for e0, e1 in GROUPS:
            load_w(e0, e1)
        pos_t = []
        for r, pos in enumerate((pos1, pos2, pos3, pos4)):
            t = keep.tile([P, T // 16], U16, name="pos_t%d" % r)
            nc.sync.dma_start(t[:], pos)
            pos_t.append(t)
        gate_last = keep.tile([P, 512], F32, name="gate_last")
        nc.sync.dma_start(out=gate_last[:], in_=gate[TOP - 1, N - P : N, 0:512])

        x_words = [keep.tile([P, T], U32, align_bytes=64, name="x_words%d" % a) for a in range(PASSES)]
        woven = {}

        def weave(a, t0, t1, on_vector):
            t = keep.tile([P, (t1 - t0) * 4], BF16, align_bytes=64, name="woven%d_%d" % (a, t0))
            dst = t[:].rearrange("p (c i j) -> p c j i", i=4, j=4)
            base = t0 - t0 % 256
            src = raw[(a, base)][:, :, t0 - base : t1 - base].rearrange("p j (c i) -> p c j i", i=4)
            if on_vector:
                nc.vector.tensor_copy(out=dst, in_=src)
            else:
                nc.scalar.activation(out=dst, in_=src, func=COPY)
            woven[(a, t0)] = t

        def quantise(a, t0, t1):
            nc.vector.quantize_mx(
                out=x_words[a][:, t0:t1].bitcast(FP8X4),
                scales=x_plane[4 * a : P, t0:t1],
                in_=woven[(a, t0)][:],
            )

        first = ((0, 256, True), (256, 512, False), (512, 640, True), (640, 768, False))
        weave(0, *first[0])
        for i in range(1, len(first)):
            weave(0, *first[i])
            quantise(0, *first[i - 1][:2])
        quantise(0, *first[-1][:2])
        for t0, t1 in X_CHUNKS[1]:
            weave(1, t0, t1, False)

        def gather_slots(window, e0, e1, dtype, name):
            t = keep.tile([P, (e1 - e0) * C], dtype, align_bytes=64, name=name)
            nc.vector.tensor_copy(t[:], window[:].indirect(offs_t[:, e0 * C // 16 : e1 * C // 16]))
            return t

        words0 = []
        for g, (e0, e1) in enumerate(GROUPS):
            words0.append(gather_slots(x_words[0], e0, e1, U32, "words0_%d" % e0))
            quantise(1, *X_CHUNKS[1][g])
        planes = []
        for g, (e0, e1) in enumerate(GROUPS):
            t = gather_slots(x_plane, e0, e1, U8, "planes%d" % e0)
            nc.scalar.dma_start(out=shifted[g][0:112, :].bitcast(I32), in_=t[4:116, :].bitcast(I32))
            planes.append(t)

        gate_cols = keep.tile([P, T // P, TOP], F32, name="gate_cols")
        for i in range(2):
            ps = bank(6 + i, "gate_ps%d" % i)
            for c in range(3):
                nc.tensor.transpose(ps[:, c * P : (c + 1) * P], gate_rows[:, (3 * i + c) * P : (3 * i + c + 1) * P], ident[:])
            nc.scalar.activation(
                out=gate_cols[:, 3 * i : 3 * i + 3, :],
                in_=ps[:, 0 : 3 * P].rearrange("p (c n) -> p c n", n=P)[:, :, 0:TOP],
                func=COPY,
            )

        words1 = {}

        def one_pass(h, e, a, acc):
            g, i = divmod(e, 4)
            cols = slice(i * C, (i + 1) * C)
            words, plane = (words0[g][:, cols], planes[g][:, cols]) if a == 0 else (words1[e], shifted[g][:, cols])
            n0 = (e * PASSES + a) * N + h * P
            nc.tensor.matmul_mx(
                out=acc,
                lhsT=w_codes[g][:, i * PASSES + a, 2 * P * h : 2 * P * (h + 1)].bitcast(FP4X4),
                lhsT_scale=w_plane[:, n0 : n0 + P],
                rhs=words.bitcast(FP8X4),
                rhs_scale=plane,
                start=(a == 0),
                stop=(a == PASSES - 1),
            )

        def activate(h, e, acc):
            nc.scalar.activation(out=y[h][:, e * C : (e + 1) * C], in_=acc, func=GELU, bias=bias[:, h, e : e + 1])

        def experts(h, e0, e1, ps):
            for e in range(e0, e1):
                for a in range(PASSES):
                    one_pass(h, e, a, ps[:, (e - e0) * C : (e - e0 + 1) * C])
            for e in range(e0, e1):
                activate(h, e, ps[:, (e - e0) * C : (e - e0 + 1) * C])

        opened = {}
        for g, (e0, e1) in enumerate(LAST_GROUPS):
            t = gather_slots(x_words[1], e0, e1, U32, "words1_%d" % e0)
            for e in range(e0, e1):
                words1[e] = t[:, (e - e0) * C : (e - e0 + 1) * C]
            if e1 == 10:
                for e in (10, 11):
                    opened[e] = bank(e - 5, "h0_%d" % e)[:, 0:C]
                    one_pass(0, e, 0, opened[e])
            if e0 in opened:
                one_pass(0, e0, 1, opened[e0])
                activate(0, e0, opened[e0])
            else:
                experts(0, e0, e1, bank(g, "h0_%d" % e0))
        for (e0, e1), i in zip((GROUPS[2], GROUPS[0], GROUPS[1]), (7, 6, 5)):
            experts(1, e0, e1, bank(i, "h1_%d" % e0))

        steps = [(h, r, u) for h in range(HALVES) for r in range(TOP) for u in range(len(PIECES))]
        steps.remove((HALVES - 1, TOP - 1, 0))
        sums = {}
        picked = {}
        scaled = {}

        def fetch(h, r, u):
            t0, t1 = PIECES[u]
            if h == HALVES - 1 and r >= TOP - 2:
                t = ring.tile([P, t1 - t0], F32, tag="picked", name="picked_piece")
                nc.vector.tensor_copy(t[:], y[h][:].indirect(pos_t[r][:, t0 // 16 : t1 // 16]))
                picked[(h, r, u)] = t[:]
            elif u == 0:
                t = ring.tile([P, T], F32, tag="picked", name="picked")
                nc.vector.tensor_copy(t[:], y[h][:].indirect(pos_t[r][:]))
                for v, (v0, v1) in enumerate(PIECES):
                    picked[(h, r, v)] = t[:, v0:v1]

        def turn_and_scale(i):
            h, r, u = steps[i]
            t0, t1 = PIECES[u]
            blocks = (t1 - t0) // P
            if i < len(steps) - 1:
                ps = bank(i % 3, "turned%d" % i)
                turned = [ps[:, c * P : (c + 1) * P] for c in range(blocks)]
            else:
                turned = [bank(3 + c, "turned_last%d" % c)[:, 0:P] for c in range(blocks)]
            for c in range(blocks):
                nc.tensor.transpose(turned[c], picked[(h, r, u)][:, c * P : (c + 1) * P], ident[:])
            t = ring.tile([P, t1 - t0], F32, tag="scaled", name="scaled")
            for c in range(blocks):
                nc.scalar.activation(
                    out=t[:, c * P : (c + 1) * P],
                    in_=turned[c],
                    func=COPY,
                    scale=gate_cols[:, t0 // P + c, r : r + 1],
                )
            scaled[i] = t

        def store(h, t0, t1, t):
            nc.sync.dma_start(out=out[h * P : (h + 1) * P, t0:t1], in_=t[:])

        def turn_back(i):
            h, r, u = steps[i]
            t0, t1 = PIECES[u]
            blocks = (t1 - t0) // P
            if r == 0:
                sums[(h, u)] = bank(((3, 4), (6, 5))[h][u], "sum%d_%d" % (h, u))
            ps = sums[(h, u)]
            last = TOP - 2 if (h, u) == (HALVES - 1, 0) else TOP - 1
            for c in range(blocks):
                nc.tensor.matmul(
                    ps[:, c * P : (c + 1) * P],
                    lhsT=scaled[i][:, c * P : (c + 1) * P],
                    rhs=ident[:],
                    is_transpose=True,
                    start=(r == 0 and c == 0),
                    stop=(r == last and c == blocks - 1),
                )
            if r == TOP - 1:
                t = keep.tile([P, t1 - t0], F32, name="result%d_%d" % (h, u))
                nc.scalar.copy(out=t[:], in_=ps[:, 0 : t1 - t0])
                store(h, t0, t1, t)

        for i, (h, r, u) in enumerate(steps):
            fetch(h, r, u)
            turn_and_scale(i)
            if i >= LAG:
                turn_back(i - LAG)
        product = ring.tile([P, 512], F32, tag="picked", name="product")
        nc.vector.tensor_tensor(
            product[:], y[HALVES - 1][:].indirect(pos_t[TOP - 1][:, 0 : 512 // 16]), gate_last[:], mybir.AluOpType.mult
        )
        for t0 in (0, 256):
            total = keep.tile([P, 256], F32, name="total%d" % t0)
            nc.vector.tensor_tensor(
                total[:], sums[(HALVES - 1, 0)][:, t0 : t0 + 256], product[:, t0 : t0 + 256], mybir.AluOpType.add
            )
            store(HALVES - 1, t0, t0 + 256, total)
        for i in range(len(steps) - LAG, len(steps)):
            turn_back(i)
